import numpy as np, ml_dtypes
CORES = [16,17,18,19,32,33,34,35]
N = 8
BF = ml_dtypes.bfloat16
def gentries(a):
    return np.ascontiguousarray(a.reshape(8, 16, -1).transpose(0, 2, 1)).reshape(8, -1)
def gtable(e):
    e = np.asarray(e); return np.ascontiguousarray(e.reshape(8, -1, 16).transpose(0, 2, 1)).reshape(128, -1).astype(np.int32)
G, C, K, RO, SH = 512, 4096, 192, 5, 9
NONE = N * G
def batch(rng, keep=(), high=()):
    key = rng.random((8, C)) * np.where(np.arange(C) >> SH == 0, 3.0, 1.0)
    for c in keep: key[:, c] += 4
    for g in high: key[g, :1 << SH] += 4
    s = np.ascontiguousarray(np.argsort(key, axis=1)[:, :N * K]); w = rng.integers(0, NONE, (8, 16, 4)); ro = np.zeros((8, 16, N * K), np.int64)
    for r in range(N):
        for t in range(16):
            if t < RO: ro[:, t, r * K:(r + 1) * K] = (r + t) % N * G + np.argsort(rng.random((8, G)), axis=1)[:, :K]
            else: ro[:, t, r * K:(r + 1) * K] = np.take_along_axis(w[:, t], rng.integers(0, 4, (8, K)), 1)
    return s, ro, w
def living(rng, s, ro, w, share):
    pa = np.full((8, 16, C), NONE, np.int64); live, dead = [], []
    for g in range(8):
        rest = rng.permutation(np.setdiff1d(np.arange(C), s[g])); h = max(int(len(rest) * share), 8)
        a = rest[h:]; m = len(a); v = rng.integers(0, NONE, (16, m))
        for k in range(RO, 16): v[k] = w[g, k][rng.integers(0, 4, m)]
        v = np.where(rng.random((16, m)) < 0.8 * rng.random((1, m)), ro[g][:, np.arange(m) % (N * K)], v)
        no = rng.random((16, m)) < 0.9 * rng.random((1, m)); no[rng.integers(0, 16, m), np.arange(m)] = False
        pa[g][:, a] = np.where(no, NONE, v); live.append(a); dead.append(rest[:h])
    return pa, live, dead
def trunks(rng, s, ro, live, dead):
    op = rng.integers(0, N * K, (N, 8, G))
    for t in rng.permutation(RO):
        for q in range(N):
            r = int((q - t) % N); np.put_along_axis(op[q], ro[:, t, r * K:(r + 1) * K] - q * G, np.ascontiguousarray(np.broadcast_to(r * K + np.arange(K), (8, K))), 1)
    tr = np.zeros((N, 8, 16, G), np.int64); sh = (N, 16, G)
    for g in range(8):
        a = live[g]; m = len(a); top = np.sort(a)[-(m >> 3):]; x = a[rng.integers(0, m, sh)]
        x = np.where(rng.random(sh) < rng.choice(np.array([0.3, 0.6, 0.8, 0.9, 1.0]), (N, 1, G)), top[rng.integers(0, len(top), sh)], x)
        x = np.where(rng.random(sh) < rng.choice(np.array([0.0, 0.1, 0.25]), (N, 1, G)), a[(op[:, g][:, None, :] + N * K * rng.integers(0, 2, sh)) % m], x)
        gone = np.concatenate([dead[g], s[g][::4]])
        tr[:, g] = np.where(rng.random(sh) < rng.choice(np.array([0.0, 0.0, 0.1, 0.3]), (N, 1, G)), gone[rng.integers(0, len(gone), sh)], x)
    return tr
def pack(tr, pa, s, ro):
    return {"trunk": np.ascontiguousarray(tr.reshape(N, 128, G)).astype(np.int32), "paths": np.stack([pa.reshape(128, C)] * N).astype(np.int32),
            "calls": np.stack([gtable(s[:, r * K:(r + 1) * K]) for r in range(N)]), "routes": np.stack([ro[:, :, r * K:(r + 1) * K].reshape(128, K) for r in range(N)]).astype(np.int32)}
def setup_inputs(rng):
    s, ro, w = batch(rng); pa, live, dead = living(rng, s, ro, w, 0.05)
    return pack(trunks(rng, s, ro, live, dead), pa, s, ro)
def setup_inputs_ties(rng):
    edge = np.array([0, C - 1] + [e for b in range(1, C >> SH) for e in ((b << SH) - 1, b << SH)])
    s, ro, w = batch(rng, edge); pa, live, dead = living(rng, s, ro, w, 0.05); tr = trunks(rng, s, ro, live, dead); sh = (N, 16, G); k = np.arange(16)[None, :, None]
    for g in range(8):
        a = np.union1d(live[g], edge); d = np.setdiff1d(np.append(dead[g], s[g][0]), edge)
        few = pa[g][:, live[g][:3]]; pa[g][:, a] = few[:, rng.integers(0, 3, len(a))]
        x = tr[:, g].copy(); x[:, 8:] = x[:, :8][:, ::-1].copy()
        kind = rng.integers(0, 5, (N, 1, G)); end = rng.choice(np.array([0, 15]), (N, 1, G)); z = a[rng.integers(0, len(a), sh)]
        x = np.where(kind == 1, edge[rng.integers(0, len(edge), sh)], np.where(kind == 2, z, x))
        tr[:, g] = np.where(kind == 3, np.where(k == end, d[rng.integers(0, len(d), sh)], z), x)
        j = rng.permutation(N * K)[:64]; r = j // K; c = rng.permutation(live[g])[:64]
        pa[g][:, c] = ro[g][:, j]; tr[r, g, rng.integers(0, 16, 64), ro[g, 0, j] - r * G] = c
        u = rng.permutation(np.setdiff1d(np.nonzero(s[g] >> SH == (C - 1) >> SH)[0], j))[:16]; q = u // K; at = ro[g, 0, u] - q * G
        b = np.sort(rng.permutation(np.setdiff1d(live[g][live[g] >> SH == 0], np.append(edge, c)))[:32].reshape(2, 16), axis=0)
        pa[g][:, b[0]] = ro[g][:, u]; pa[g][:, b[1]] = ro[g][:, u]; h = rng.integers(0, 16, 16)
        pa[g, h, b[0]] = np.where(rng.random(16) < 0.5, NONE, (ro[g, h, u] + 1) % NONE)
        y = tr[:, g]; e = rng.integers(0, 16, 16)
        y[q, :, at] = b[rng.integers(0, 2, (16, 16)), np.arange(16)[:, None]]
        y[q, e, at] = b[1]; y[q, (e + 8) & 15, at] = b[0]
    return pack(tr, pa, s, ro)
def setup_inputs_same(rng):
    few = np.array([0, 1, 2, (1 << SH) - 1]); keep = np.append(few, C - 1)
    s, ro, w = batch(rng, keep, (5, 6, 7)); pa, live, dead = living(rng, s, ro, w, 0.05); tr = trunks(rng, s, ro, live, dead); sh = (N, 16, G)
    for g in range(8):
        pa[g][:, keep] = ro[g][:, rng.integers(0, N * K, len(keep))]
        top = np.union1d(live[g][live[g] >> SH == (C - 1) >> SH], np.array([C - 1])); x = top[rng.integers(0, len(top), sh)]
        if g > 4:
            low = rng.permutation(live[g][live[g] >> SH == 0]); n = rng.permutation(N * K); q = np.arange(N * K) // K; at = ro[g, 0] - q * G
            if g == 5: i = (n >= 256).astype(np.int64) + (n >= 768)
            elif g == 6: i = (n >= 1024).astype(np.int64)
            else: i = np.arange(N * K) % len(low)
            y = np.where(tr[:, g] >> SH == 0, x, tr[:, g]); y[q, :, at] = x[q, :, at]
            y[q, rng.integers(0, 16, N * K), at] = low[i]; tr[:, g] = y
            continue
        one = few[rng.integers(0, (1, 2, 4)[g % 3], (N, 1, G))]
        x = np.where(np.arange(16)[None, :, None] == rng.integers(0, 16, (N, 1, G)), one, x)
        tr[:, g] = np.where(rng.random((N, 1, G)) < (1.0 if g < 4 else 0.6), x, tr[:, g])
    return pack(tr, pa, s, ro)
def setup_inputs_block(rng):
    s, ro, w = batch(rng, [C - 1]); o = rng.permutation(8); f = int(o[4])
    if not np.any(s[f] == 0): s[f, int(rng.integers(0, N * K))] = 0
    for r in range(N):
        p = rng.permutation(G); v = (r - 1) % N
        ro[f, 0, r * K:(r + 1) * K] = r * G + p[:K]; ro[f, 1, v * K:(v + 1) * K] = r * G + p[K:2 * K]
    pa, live, dead = living(rng, s, ro, w, 0.05); tr = trunks(rng, s, ro, live, dead); sh = (N, 16, G); q = int(rng.integers(0, N))
    for h in range(5):
        g = int(o[h]); pa[g][:, C - 1] = ro[g][:, 0]
        top = np.union1d(live[g][live[g] >> SH == (C - 1) >> SH], np.array([C - 1])); d = np.setdiff1d(dead[g], np.array([C - 1]))
        full = top[rng.integers(0, len(top), sh)]; free = d[rng.integers(0, len(d), sh)]
        if h == 0: tr[:, g] = full
        if h == 1 or h == 2: tr[:, g] = free
        if h == 2: tr[q, g] = full[q]
        if h == 3: pa[g] = NONE
        if h == 4:
            a = np.arange(N * K) // K; b = (a + 1) % N; u = ro[g, 0] - a * G; v = ro[g, 1] - b * G; y = tr[:, g]
            y[a, rng.integers(0, 16, N * K), u] = d[rng.integers(0, len(d), N * K)]
            y[b, :, v] = full[b, :, v]; y[b[::4], rng.integers(0, 16, len(b[::4])), v[::4]] = s[g][::4]
    return pack(tr, pa, s, ro)
def setup_inputs_late(rng):
    s, ro, w = batch(rng); pa, live, dead = living(rng, s, ro, w, 0.05); tr = trunks(rng, s, ro, live, dead); sh = (N, 16, G)
    for g in range(8):
        tr[:, g] = np.where(rng.random(sh) < rng.choice(np.array([0.0, 0.5, 1.0]), (N, 1, G)), s[g][rng.integers(0, N * K, sh)], tr[:, g])
        u = np.argsort(s[g, :K])[:16]; v = K + np.argsort(s[g, K:2 * K])[-16:]
        y = tr[2, g]; y[:, ro[g, 1, v] - 2 * G] = s[g][u]
        for a, r, t in ((u, 0, 0), (v, 1, 0), (u, 0, 1)):
            y = tr[r + t, g]; y[:2, ro[g, t, a] - (r + t) * G] = dead[g][0]
        e = np.argsort(s[g, :K])[16:]; e = e[np.isin(ro[g, 1, e], ro[g, 0, K:2 * K], invert=True)]; lo, hi = e[:16], e[-16:]
        top = live[g][live[g] >> SH == (C - 1) >> SH]
        assert len(e) >= 32 and len(top) > 0 and np.all((s[g][lo] >> SH) < (s[g][hi] >> SH))
        assert np.all(np.any(pa[g][:, top] != NONE, axis=0)) and np.all(pa[g][:, dead[g][0]] == NONE)
        y = tr[0, g]; y[:2, ro[g, 0, np.append(lo, hi)]] = dead[g][0]
        y = tr[1, g]; y[:, ro[g, 1, lo] - G] = top[rng.integers(0, len(top), 16)]; y[:, ro[g, 1, hi] - G] = s[g][lo]
    return pack(tr, pa, s, ro)
def setup_inputs_spread(rng):
    s, ro, w = batch(rng); late = ro[:, RO:]; ro[:, RO:] = np.where(rng.random(late.shape) < 0.5, rng.integers(0, NONE, late.shape), late)
    pa, live, dead = living(rng, s, ro, w, 0.02); tr = trunks(rng, s, ro, live, dead)
    pa = np.where((pa != NONE) & (rng.random(pa.shape) < 0.5), np.minimum((NONE * rng.random(pa.shape) ** 4).astype(np.int64), NONE - 1), pa)
    x = np.minimum((C * rng.random(tr.shape) ** rng.choice(np.array([0.25, 1.0, 4.0]), (N, 8, 1, G))).astype(np.int64), C - 1)
    return pack(np.where(rng.random((N, 8, 1, G)) < 0.5, x, tr), pa, s, ro)
def check_inputs(d):
    bad = []
    for k, lo, hi in (("trunk", 0, C - 1), ("paths", 0, NONE), ("calls", 0, C - 1), ("routes", 0, NONE - 1)):
        if np.min(d[k]) < lo or np.max(d[k]) > hi: bad.append("range of " + k)
    if bad: return bad
    if np.any(d["paths"] != d["paths"][:1]): bad.append("paths alike on all ranks")
    s = np.concatenate([gentries(a) for a in d["calls"]], axis=1).astype(np.int64)
    if np.any(np.diff(np.sort(s, axis=1), axis=1) == 0): bad.append("calls of a group all different")
    if np.any(np.take_along_axis(d["paths"][0].reshape(8, 16, C), s[:, None, :], 2) != NONE): bad.append("paths of the seekers are none")
    own = (np.arange(N)[:, None] + np.arange(RO)[None, :]) % N
    at = d["routes"].astype(np.int64).reshape(N, 8, 16, K)[:, :, :RO] - own[:, None, :, None] * G
    if np.min(at) < 0 or np.max(at) > G - 1: bad.append("row t of routes names bundles of rank (r + t) mod N")
    if np.any(np.diff(np.sort(at, axis=3), axis=3) == 0): bad.append("row t of routes names different bundles")
    return bad
def reference(trunk, paths, calls, routes):
    tr = trunk.astype(np.int64).reshape(N, 8, 16, G); pa = paths[0].astype(np.int64).reshape(8, 16, C)
    sl = np.stack([gentries(a) for a in calls]).astype(np.int64); ro = routes.astype(np.int64).reshape(N, 8, 16, K)
    row = np.arange(16)[None, :, None]; D = C // N
    for t in range(RO):
        new = pa.copy(); gone = np.zeros((8, C), bool)
        for q in range(N):
            r = (q - t) % N; s = sl[r]; at = ro[r, :, t] - q * G
            hold = np.take_along_axis(tr[q], at[:, None, :], 2)
            hop = np.take_along_axis(pa, hold.reshape(8, 1, 16 * K), 2).reshape(8, 16, 16, K)
            dead = np.logical_not(np.any(hop != NONE, axis=1))
            like = np.add.reduce((hop == ro[r][:, :, None, :]).astype(np.int64), axis=1)
            may = (hold >> SH) < (s >> SH)[:, None, :]
            key = np.where(dead, 2 ** 22 + 15 - row, np.where(may, (like * C + C - 1 - hold) * 16 + 15 - row, -1))
            best = np.max(key, axis=1); p = 15 - (best & 15)
            go = np.any(np.take_along_axis(pa, s[:, None, :], 2) != NONE, axis=1) | (t == 0)
            won = go & (best >= 0); vic = np.take_along_axis(hold, p[:, None, :], 1)[:, 0]
            b, i = np.nonzero(won); tr[q, b, p[b, i], at[b, i]] = s[b, i]; new[b, t, s[b, i]] = ro[r, b, t, i]
            b, i = np.nonzero(won & (best < 2 ** 22)); gone[b, vic[b, i]] = True
            b, i = np.nonzero(go & (best < 0)); gone[b, s[b, i]] = True
        pa = np.where(gone[:, None, :], NONE, new)
    return {"yt": tr.reshape(N, 128, G).astype(np.float32), "yp": np.stack([pa[:, :, r * D:(r + 1) * D].reshape(128, D) for r in range(N)]).astype(np.float32)}

from concourse.bass import DstId, RemoteDMATransfer
from concourse.mybir import AluOpType, ActivationFunctionType

RO = 5
F32, BF, I32, U16 = "float32", "bfloat16", "int32", "uint16"
SCRATCH = {}


def _b(where, dtype, **kw):
    for k, s in kw.items():
        SCRATCH[k] = (where, s, dtype)


_b("dram", I32, stR=[8, 128, 24], stC=[8, 128, 2], stT=[8, 128, 64], landR=[8, 128, 24], landC=[8, 128, 2], landT=[8, 128, 64])
_b("dram", F32, stV=[8, 128, 64], landV=[8, 128, 64], stY=[8, 128, 64], landY=[8, 128, 64])
_b("dram", BF, stD=[8, 128, 4], landD=[8, 128, 4])
_b("sbuf", I32, P=[128, 4096], XP=[64, 1024], P2=[128, 512], ii=[128, 192], col=[128, 256], cp=[128, 1], ci=[128, 4],
   cq8=[128, 256], iia=[128, 192], cola=[128, 192], t12b=[128, 12], Cl=[128, 12], Cti=[128, 12], R=[128, 192],
   OT=[128, 60], Tki=[128, 512], BI=[128, 12], UI=[128, 24], C2=[128, 12], NI=[128, 12], NI2=[128, 24], RI=[128, 192],
   RIh=[128, 192], RIl=[128, 192], ccq=[128, 128])
_b("sbuf", U16, LI=[128, 12], LB=[128, 12], AT=[128, 60], SN=[128, 60], H16=[128, 192])
_b("sbuf", F32, KC=[128, 16], IDf=[128, 128], I64s=[128, 64], REPf=[128, 256], SELq=[128, 16], EM=[128, 192], DM=[128, 192],
   REP8=[8, 128], Clf=[128, 12], Cs=[128, 12], Ctf=[128, 12], E=[128, 192], Es=[128, 192], Et=[128, 192],
   SG=[128, 960], TH=[128, 960], RJ=[128, 960], RA=[128, 3072], RB=[128, 3072], Tk=[128, 512], Hf=[128, 192],
   Dg=[128, 192], M=[128, 192], A1=[128, 192], KEY=[128, 192], KB=[128, 192], T1=[128, 96], T2=[128, 48], T3=[128, 24],
   BEST=[128, 12], BW=[128, 8], Bm=[128, 8], bT=[8, 192], W=[128, 192], UF=[128, 24], OK=[128, 12], NF=[128, 24],
   S0=[128, 192], S1=[128, 96], S2=[128, 48], S3=[128, 24], S4=[128, 12], VAL=[128, 512], VR=[128, 512], YP=[128, 512])
_b("sbuf", BF, iot=[128, 64], iotR=[128, 64], WST=[128, 144], W0=[128, 144], DW=[128, 2048], OUTW=[128, 128], YS=[128, 240],
   YS64=[128, 240], R8b=[8, 128], ID64=[64, 64], F=[128, 4096], ZA=[128, 4096], ZB=[128, 4096], EQ=[128, 3072], FG=[128, 3072],
   FS=[128, 192], OHI=[128, 768], OLO=[128, 768], SHI=[128, 768], SLO=[128, 768], D=[64, 64], ZVa=[128, 192], ZVb=[128, 192],
   KD=[8, 512])
_b("psum", F32, KPa=[128, 512], KPb=[128, 512], pBa=[128, 512], pBb=[128, 512], pTR=[128, 512], pD=[128, 512], pM=[128, 512],
   pZ=[128, 512])

_ARR = ["arrR", "arrC", "arrT", "arrV", "arrY", "arrD"]
_DMA = ["dR", "dC", "dT", "dP", "dX", "dP2", "dF", "dCl", "dRl", "dO", "dTk", "dRR", "dRJ", "dSN", "dV", "dVR", "dY", "dD", "dKD",
        "oY1", "oY2", "oP"]
SEMAPHORES = ["cv", "cs", "cpe", "cg", "sent"] + _ARR + _DMA


def rank_program(g, core, T, topo):
    me = T.rank_of(core)
    if me is None:
        return
    A, AF = AluOpType, ActivationFunctionType
    eng = {"v": g.vector, "s": g.scalar, "p": g.tensor, "g": g, "y": g.sync}
    own = {"v": "cv", "s": "cs", "p": "cpe", "g": "cg"}
    cnt = {s: 0 for s in SEMAPHORES}
    seen = {q: {} for q in eng}

    def need(q, deps):
        best = {}
        for d in deps:
            if d is not None:
                best[d[0]] = max(best.get(d[0], 0), d[1])
        for s, n in best.items():
            if seen[q].get(s, 0) < n:
                eng[q].wait_ge(T.sem[s], n)
                seen[q][s] = n

    def op(q, f, *deps):
        need(q, deps)
        s = own[q]
        f(eng[q]).then_inc(T.sem[s], 1)
        cnt[s] += 1
        return (s, cnt[s])

    def V(f, *deps):
        return op("v", f, *deps)

    def S(f, *deps):
        return op("s", f, *deps)

    def MM(deps, *ms):
        need("p", deps)
        for n, m in enumerate(ms):
            i = eng["p"].matmul(m[0], m[1], m[2], start=m[3], stop=m[4])
            if n == len(ms) - 1:
                i.then_inc(T.sem["cpe"], 1)
        cnt["cpe"] += 1
        return ("cpe", cnt["cpe"])

    def dma(q, out, in_, sem, *deps):
        need(q, deps)
        eng[q].dma_start(out, in_).then_inc(T.sem[sem], 16)
        cnt[sem] += 16
        return (sem, cnt[sem])

    def ts(out, in0, s1, op0, s2=None, op1=None):
        if op1 is None:
            return lambda e: e.tensor_scalar(out, in0, s1, None, op0)
        return lambda e: e.tensor_scalar(out, in0, s1, s2, op0, op1)

    def tt(out, a, b, o):
        return lambda e: e.tensor_tensor(out, a, b, o)

    def cpy(out, in_):
        return lambda e: e.tensor_copy(out, in_)

    def act(out, in_, f=AF.Copy):
        return lambda e: e.activation(out, in_, f)

    def send(src, dst, sem, *deps):
        need("g", deps)
        order = sorted([(me + k) % 8 for k in range(1, 8)], key=lambda n: len(topo.engines(core, T.cores[n])))
        used, tr = [], []
        for n in order:
            c = T.cores[n]
            es = [e for e in topo.engines(core, c) if e not in used][:2]
            used += es
            a = topo.addr(c)
            tr.append(RemoteDMATransfer(dst_ids=[DstId(rid=a[0], pnc=a[1])], dma_engine_mask=sum(1 << e for e in es),
                                        remote_sem=T.sem[sem], srcs=[T[src][n]], dsts=[T[dst][me]], alu_op=0))
        g.remote_dma_fused(tr, local_sem=T.sem["sent"])
        cnt["sent"] += 14
        cnt[sem] += 14

    lo, hi = 16 * me, 16 * me + 16
    dma("y", T.stC[:, 0:96, :], T.calls[:], "dC")
    dma("y", T.stC[:, 96:128, :], T.trunk[0:1, :], "dC")
    tC = dma("y", T.landC[me, 0:96, :], T.calls[lo:hi, :], "dC")
    dma("y", T.stR[:], T.routes[:], "dR")
    tR = dma("y", T.landR[me], T.routes[lo:hi, :], "dR")
    dma("y", T.stT[:], T.trunk[:], "dT")
    tT = dma("y", T.landT[me], T.trunk[lo:hi, :], "dT")
    for q in range(8):
        tP = dma("s", T.P[16 * q:16 * q + 16, :], T.paths[lo:hi, :], "dP")
    for k in range(16):
        tX = dma("y", T.XP[:, 64 * k:64 * k + 64], T.paths[lo + k:lo + k + 1, :], "dX")
    for q in range(8):
        tP2 = dma("s", T.P2[16 * q:16 * q + 16, :], T.paths[lo:hi, 512 * q:512 * q + 512], "dP2")
    g1 = op("g", lambda e: e.iota(T.cp[:, 0:1], [[0, 1]], 0, 1))
    g2 = op("g", lambda e: e.iota(T.col[:, :], [[1, 256]], 0, 0))
    g3 = op("g", lambda e: e.iota(T.ii[:, :], [[1, 12], [12, 16]], 0, 0))
    send("stC", "landC", "arrC", tC)
    send("stR", "landR", "arrR", tR)
    send("stT", "landT", "arrT", tT)
    gz = op("g", lambda e: e.iota(T.ZA[:, :], [[0, 4096]], 0, 0, allow_small_or_imprecise_dtypes=True))
    gz = op("g", lambda e: e.iota(T.ZB[:, :], [[0, 4096]], 0, 0, allow_small_or_imprecise_dtypes=True))

    vF = V(lambda e: e.memset(T.F[:, :], 0.0))
    V(lambda e: e.memset(T.Bm[:, :], 0.0))
    KC, col, ci = T.KC, T.col, T.ci

    def kc(n):
        return KC[:, n:n + 1]
    V(ts(ci[:, 0:1], T.cp[:, 0:1], 15, A.bitwise_and), g1)
    V(ts(ci[:, 1:2], T.cp[:, 0:1], 4, A.arith_shift_right))
    V(ts(ci[:, 2:3], T.cp[:, 0:1], 63, A.bitwise_and))
    V(cpy(kc(0), T.cp[:, 0:1]))
    v = V(ts(T.cq8[:, :], col[:, :], 4, A.arith_shift_right, 7, A.bitwise_and), g2)
    V(ts(T.cola[:, :], col[:, 0:192], 15, A.bitwise_and))
    V(ts(T.iia[:, :], T.ii[:, :], 15, A.bitwise_and), g3)
    V(ts(T.ccq[:, 0:16], col[:, 0:16], 7, A.bitwise_and))
    V(cpy(kc(1), ci[:, 0:1]), v)
    V(cpy(kc(2), ci[:, 1:2]))
    V(cpy(kc(7), ci[:, 2:3]))
    V(ts(kc(3), ci[:, 1:2], 512.0, A.mult))
    V(ts(kc(4), ci[:, 1:2], 16.0, A.mult, 15.0, A.add))
    V(ts(kc(8), ci[:, 0:1], 112.0, A.add))
    V(ts(kc(9), ci[:, 0:1], -1.0, A.mult, float(2 ** 21 + 15), A.add))
    V(ts(kc(10), ci[:, 0:1], 5.0, A.is_lt))
    V(ts(kc(11), ci[:, 0:1], 0.0, A.is_equal))
    V(ts(kc(12), ci[:, 1:2], 16.0, A.mult, 16.0, A.add))
    V(ts(kc(14), ci[:, 0:1], 12.0, A.mult))
    v = V(ts(kc(13), ci[:, 1:2], 1.0, A.add))
    V(tt(kc(12), kc(12), kc(11), A.mult), v)
    v = V(tt(kc(13), kc(13), kc(11), A.mult))
    V(ts(kc(5), kc(12), -1.0, A.add), v)
    v = V(ts(kc(6), kc(13), -1.0, A.add))
    V(ts(T.WST[:, :], col[:, 0:144], kc(4), A.is_equal, 65536.0, A.mult), v)
    V(ts(T.W0[:, :], col[:, 0:144], kc(5), A.is_equal))
    v = V(ts(T.t12b[:, :], col[:, 0:12], kc(14), A.add))
    V(cpy(T.LI[:, :], T.t12b[:, :]), v)
    v = V(ts(T.Cti[:, :], T.t12b[:, :], 4, A.arith_shift_right))
    vLB = V(cpy(T.LB[:, :], T.Cti[:, :]), v)
    V(ts(T.IDf[:, :], col[:, 0:128], kc(0), A.is_equal))
    V(ts(T.ID64[:, :], col[0:64, 0:64], KC[0:64, 0:1], A.is_equal))
    V(ts(T.I64s[:, :], col[:, 0:64], kc(7), A.is_equal))
    V(ts(T.REPf[:, :], T.cq8[:, :], kc(2), A.is_equal))
    V(ts(T.SELq[:, :], T.ccq[:, 0:16], kc(2), A.is_equal))
    V(ts(T.EM[:, :], T.iia[:, :], kc(1), A.is_equal))
    V(ts(T.DM[:, :], T.cola[:, :], kc(1), A.is_equal))
    V(ts(T.REP8[:, :], T.cq8[0:8, 0:128], KC[0:8, 0:1], A.is_equal))
    V(ts(T.R8b[:, :], T.cq8[0:8, 0:128], KC[0:8, 0:1], A.is_equal, 4096.0, A.mult))
    V(ts(T.OUTW[:, :], T.cq8[:, 0:128], kc(6), A.is_equal, -float(2 ** 27), A.mult))
    V(ts(T.YS[:, :], col[:, 0:240], kc(8), A.is_equal))
    V(ts(T.YS64[:, :], col[:, 0:240], kc(8), A.is_equal, 64.0, A.mult))
    V(cpy(T.iot[:, :], col[:, 0:64]))
    V(ts(T.iotR[:, :], col[:, 0:64], -1.0, A.mult, 63.0, A.add))
    for p in range(16):
        vC = V(ts(T.DW[:, 128 * p:128 * p + 128], T.W0[:, 15 - p:143 - p], float(2 ** 22 * (16 - p)), A.mult))
    v, n = tX, 512
    while n >= 64:
        v = V(tt(T.XP[:, 0:n], T.XP[:, 0:n], T.XP[:, n:2 * n], A.min), v)
        n //= 2
    vD = V(ts(T.D[:, :], T.XP[:, 0:64], 4096.0, A.is_ge), v)

    def flags_to_F(tok):
        for q in range(8):
            t = dma("y", T.F[16 * q:16 * q + 1, :], T.D[:, :], "dF", tok)
        return t
    need("y", [("arrC", 14), tC])
    tCl = dma("y", T.Cl[:, :], T.landC[:, 0:96, :], "dCl")
    need("y", [("arrR", 14), tR])
    tRl = dma("y", T.R[:, :], T.landR[:], "dRl")
    for t in range(RO):
        tO = dma("y", T.OT[16 * t:128, 12 * t:12 * t + 12], T.landR[0:8 - t, 8 * t:8 * t + 8, :], "dO")
        if t:
            tO = dma("y", T.OT[0:16 * t, 12 * t:12 * t + 12], T.landR[8 - t:8, 8 * t:8 * t + 8, :], "dO")
    need("y", [("arrT", 14), tT])
    tTk = dma("y", T.Tki[:, :], T.landT[:], "dTk")
    tF = flags_to_F(vD)

    v = V(cpy(T.Clf[:, :], T.Cl[:, :]), tCl, vC, vLB)
    V(ts(T.Cti[:, :], T.Cl[:, :], 3584, A.bitwise_and))
    v = V(ts(T.Cs[:, :], T.Cl[:, :], -16.0, A.mult, 65520.0, A.add))
    V(cpy(T.Ctf[:, :], T.Cti[:, :]), v)
    vE = V(tt(T.E[:, :], T.Clf[:, :].indirect(T.LB[:, :]), T.EM[:, :], A.mult))
    V(tt(T.Es[:, :], T.Cs[:, :].indirect(T.LB[:, :]), T.EM[:, :], A.mult))
    vE = V(tt(T.Et[:, :], T.Ctf[:, :].indirect(T.LB[:, :]), T.EM[:, :], A.mult), vE)
    vRJ = V(cpy(T.RJ[:, 0:192], T.R[:, :].indirect(T.LI[:, :])), tRl)
    pn = MM([vE], (T.pBa[:, 0:8], T.E[:, 0:128], T.SELq[:, 8:16], True, True),
            (T.pBa[0:64, 8:12], T.E[:, 128:192], T.SELq[:, 8:12], True, True),
            (T.pBa[64:128, 8:12], T.E[:, 128:192], T.SELq[:, 12:16], True, True))

    def rep(t):
        return T.REPf[:, 16 * (8 - t):16 * (16 - t)]
    sprep = [None] * RO

    def prep(t):
        m = MM([vE, sprep[t - 1] if t else None], (T.pM[:, 0:192], rep(t), T.E[:, :], True, True),
               (T.pM[:, 192:384], rep(t), T.Et[:, :], True, True))
        S(act(T.SG[:, 192 * t:192 * t + 192], T.pM[:, 0:192]), m)
        sprep[t] = S(act(T.TH[:, 192 * t:192 * t + 192], T.pM[:, 192:384]))

    rr = [None] * RO
    RRb = [T.RA, T.RB]
    for p in range(8):
        a = V(cpy(T.RA[:, p::16], T.RJ[:, 0:192]), vRJ)
        b = S(act(T.RA[:, 8 + p::16], T.RJ[:, 0:192]), vRJ)
    rr[0] = [a, b]
    prep(0)
    vNI = V(cpy(T.NI[:, :], T.pBa[:, 0:12]), pn)
    vAT = V(ts(T.AT[:, :], T.OT[:, :], kc(3), A.subtract), tO)
    vTk = V(cpy(T.Tk[:, :], T.Tki[:, :]), tTk)
    dma("y", T.RB[16:128, :], T.RA[0:112, :], "dRR", *rr[0])
    rr[1] = [dma("y", T.RB[0:16, :], T.RA[112:128, :], "dRR")]
    for t in (2, 3, 4):
        dma("y", T.RJ[16 * t:128, 192 * t:192 * t + 192], T.RJ[0:128 - 16 * t, 0:192], "dRJ", vRJ)
        tRJ = dma("y", T.RJ[0:16 * t, 192 * t:192 * t + 192], T.RJ[128 - 16 * t:128, 0:192], "dRJ")
    tSN = None
    vD1 = vD

    def zmm(half):
        z, w = (T.ZA, T.YS64) if half == 0 else (T.ZB, T.YS)
        return MM([vZ], *[(T.pZ[:, :], w[:, 112 - 16 * q:240 - 16 * q], z[:, 512 * q:512 * q + 512], half == 0 and q == 0,
                          half == 1 and q == 7) for q in range(8)])

    for t in range(RO):
        at = T.AT[:, 12 * t:12 * t + 12]
        RR = RRb[t % 2]
        SGt, THt = T.SG[:, 192 * t:192 * t + 192], T.TH[:, 192 * t:192 * t + 192]
        h16 = V(cpy(T.H16[:, :], T.Tk[:, :].indirect(at)), vTk, vAT)
        hf = S(act(T.Hf[:, :], T.Tk[:, :].indirect(at)), vTk, vAT)

        def eq(c):
            return V(tt(T.EQ[:, 1024 * c:1024 * c + 1024], T.P[:, :].indirect(T.H16[:, 64 * c:64 * c + 64]),
                        RR[:, 1024 * c:1024 * c + 1024], A.is_equal), h16, tP, *rr[t])

        def fg(q, c):
            o, w = T.FG[:, 1024 * c:1024 * c + 1024], T.F[:, :].indirect(T.H16[:, 64 * c:64 * c + 64])
            return op(q, act(o, w) if q == "s" else cpy(o, w), h16, tF, vF)
        if t < 4:
            prep(t + 1)
        if 1 <= t < 4:
            for p in range(16):
                x = S(act(RRb[(t + 1) % 2][:, p::16], T.RJ[:, 192 * (t + 1):192 * (t + 2)]), tRJ, *rr[t])
            rr[t + 1] = [x]
        e0 = eq(0)
        v = V(tt(T.Dg[:, :], SGt, T.Hf[:, :], A.subtract), hf, sprep[t])
        vM = V(tt(T.M[:, :], T.Hf[:, :], THt, A.is_lt))
        e1 = eq(1)
        sA = S(lambda e: e.activation(T.A1[:, :], T.Dg[:, :], AF.Identity, bias=kc(9), scale=16.0), v)
        f0 = fg("s", 0)
        f1 = fg("s", 1)
        if t:
            fs = S(act(T.FS[:, :], T.F[:, :].indirect(T.SN[:, 12 * t:12 * t + 12])), tSN)
        e2 = eq(2)
        vA = V(tt(T.A1[:, :], T.M[:, :], T.A1[:, :], A.mult), sA, vM)
        f2 = fg("v" if t else "s", 2)

        def dst(c):
            return T.KPb[:, 0:64] if c == 2 else T.KPa[:, 64 * c:64 * c + 64]

        def eqm(c, tok):
            return MM([tok], *[(dst(c), T.WST[:, 15 - p:143 - p], T.EQ[:, 1024 * c + p:1024 * c + 1024:16], False, False)
                               for p in range(16)])

        def fgm(c, tok, last):
            return MM([tok], *[(dst(c), T.DW[:, 128 * p:128 * p + 128], T.FG[:, 1024 * c + p:1024 * c + 1024:16], False,
                                last and p == 15) for p in range(16)])
        MM([vE], (T.KPa[:, 0:128], rep(t), T.Es[:, 0:128], True, False))
        MM([vE], (T.KPb[:, 0:64], rep(t), T.Es[:, 128:192], True, False))
        eqm(0, e0)
        eqm(1, e1)
        eqm(2, e2)
        fgm(0, f0, False)
        pa = fgm(1, f1, t == 0)
        if t:
            pa = MM([fs], (T.KPa[:, 0:128], T.OUTW[:, :], T.FS[:, 0:128], False, True))
            MM([fs], (T.KPb[:, 0:64], T.OUTW[:, :], T.FS[:, 128:192], False, False))
        pb = fgm(2, f2, True)
        ka = V(tt(T.KEY[:, 0:128], T.KPa[:, 0:128], T.A1[:, 0:128], A.add), pa, vA)
        kb = V(tt(T.KEY[:, 128:192], T.KPb[:, 0:64], T.A1[:, 128:192], A.add), pb)
        xa = MM([ka], (T.pBa[:, 0:128], T.KEY[:, 0:128], T.IDf[:, :], True, True))
        sa = S(act(T.KB[:, 0:128], T.pBa[:, 0:128]), xa)
        xb = MM([kb], (T.pBb[0:64, 0:64], T.KEY[:, 128:192], T.IDf[:, 0:64], True, True),
                (T.pBb[64:128, 0:64], T.KEY[:, 128:192], T.IDf[:, 64:128], True, True))
        sb = S(act(T.KB[:, 128:192], T.pBb[:, 0:64]), xb)
        if t == 0:
            v = V(tt(T.S0[:, :], SGt, T.DM[:, :], A.mult))
            for x, y in ((T.S0, T.S1), (T.S1, T.S2), (T.S2, T.S3), (T.S3, T.S4)):
                v = V(tt(y[:, :], x[:, 0::2], x[:, 1::2], A.add), v)
            vSN = V(cpy(T.SN[:, 0:12], T.S4[:, :]), v)
            for u in range(1, RO):
                dma("y", T.SN[16 * u:128, 12 * u:12 * u + 12], T.SN[0:128 - 16 * u, 0:12], "dSN", vSN)
                tSN = dma("y", T.SN[0:16 * u, 12 * u:12 * u + 12], T.SN[128 - 16 * u:128, 0:12], "dSN")
            V(ts(T.NI2[:, 0:12], T.NI[:, :], 6, A.arith_shift_right), vNI)
            v = V(ts(T.NI2[:, 12:24], T.NI[:, :], 63, A.bitwise_and))
            v = V(cpy(T.NF[:, :], T.NI2[:, :]), v)
            for c in range(12):
                V(ts(T.SHI[:, 64 * c:64 * c + 64], T.iot[:, :], T.NF[:, c:c + 1], A.is_equal), v)
                vS = V(ts(T.SLO[:, 64 * c:64 * c + 64], T.iot[:, :], T.NF[:, 12 + c:13 + c], A.is_equal, -1.0, A.mult))
        if t == 1:
            v = V(cpy(T.RI[:, :], T.RJ[:, 0:192]))
            V(ts(T.RIh[:, :], T.RI[:, :], 6, A.arith_shift_right), v)
            v = V(ts(T.RIl[:, :], T.RI[:, :], 63, A.bitwise_and))
            V(ts(T.ZVa[:, :], T.RIh[:, :], -64.0, A.add, kc(10), A.mult), v)
            v = V(ts(T.ZVb[:, :], T.RIl[:, :], kc(10), A.mult))
            V(cpy(T.ZA[:, :].indirect(T.SN[:, 0:12]), T.ZVa[:, :]), v, gz)
            vZ = V(cpy(T.ZB[:, :].indirect(T.SN[:, 0:12]), T.ZVb[:, :]))
        if t == 3:
            vV = V(tt(T.VAL[:, :], T.pZ[:, :], T.P2[:, :], A.add), pz, tP2)
            dma("y", T.stV[:], T.VAL[:, :], "dV", vV)
            tV = dma("y", T.landV[me], T.VAL[lo:hi, :], "dV")
            send("stV", "landV", "arrV", tV)
        v = V(tt(T.T1[:, :], T.KB[:, 0::2], T.KB[:, 1::2], A.max), sa, sb)
        v = V(tt(T.T2[:, :], T.T1[:, 0::2], T.T1[:, 1::2], A.max), v)
        v = V(tt(T.T3[:, :], T.T2[:, 0::2], T.T2[:, 1::2], A.max), v)
        vb = V(tt(T.BEST[:, :], T.T3[:, 0::2], T.T3[:, 1::2], A.max), v)
        vi = V(tt(T.BI[:, :], T.T3[:, 0::2], T.T3[:, 1::2], A.max))
        w = float(2 ** 21) - 0.5
        V(ts(T.BW[:, :], T.BEST[:, 0:8], w, A.max), vb)
        V(ts(T.Bm[0:64, 0:4], T.BEST[0:64, 8:12], w, A.max))
        v = V(ts(T.Bm[64:128, 4:8], T.BEST[64:128, 8:12], w, A.max))
        m = MM([v], (T.pTR[0:8, 0:128], T.BW[:, :], T.IDf[:, :], True, True),
               (T.pTR[0:8, 128:192], T.Bm[:, :], T.I64s[:, :], True, True))
        sT = S(act(T.bT[:, :], T.pTR[0:8, 0:192]), m)
        pR = MM([sT], (T.pTR[:, 192:384], T.REP8[:, :], T.bT[:, :], True, True))
        V(ts(T.UI[:, 0:12], T.BI[:, :], 10, A.arith_shift_right, 63, A.bitwise_and), vi)
        V(ts(T.UI[:, 12:24], T.BI[:, :], 4, A.arith_shift_right, 63, A.bitwise_and))
        v = V(ts(T.C2[:, :], T.BI[:, :], 22, A.arith_shift_right))
        V(cpy(T.UF[:, :], T.UI[:, :]), v)
        v = V(ts(T.OK[:, :], T.C2[:, :], 0.0, A.is_equal))
        ms = [(T.pD[0:64, 0:64], T.ID64[:, :], T.D[:, :], True, False)]
        if t == 0:
            ms += [(T.pD[0:64, 0:64], T.SHI[:, 64 * c:64 * c + 64], T.SLO[:, 64 * c:64 * c + 64], False, False) for c in range(12)]
        MM([vD1, vS], *ms)
        for c in range(12):
            V(ts(T.OHI[:, 64 * c:64 * c + 64], T.iotR[:, :], T.UF[:, c:c + 1], A.is_equal, T.OK[:, c:c + 1], A.mult), v)
            x = V(ts(T.OLO[:, 64 * c:64 * c + 64], T.iotR[:, :], T.UF[:, 12 + c:13 + c], A.is_equal))
            pd = MM([x], (T.pD[0:64, 0:64], T.OHI[:, 64 * c:64 * c + 64], T.OLO[:, 64 * c:64 * c + 64], False, c == 11))
        vD1 = S(act(T.D[:, :], T.pD[0:64, 0:64], AF.Sign), pd)
        if t < 4:
            tF = flags_to_F(vD1)
        v = V(tt(T.W[:, :], T.pTR[:, 192:384], T.KEY[:, :], A.is_equal), pR)
        v = V(tt(T.W[:, :], T.W[:, :], T.Dg[:, :], A.mult), v)
        vTk = V(lambda e: e.tensor_tensor(T.Tk[:, :].indirect(at), T.Hf[:, :], T.W[:, :], A.add), v)
        if t in (1, 2):
            pz = zmm(t - 1)
    dma("y", T.stD[:], T.D[:, :], "dD", vD1)
    tD = dma("y", T.landD[me], T.D[8 * me:8 * me + 8, :], "dD")
    tY = dma("y", T.stY[:], T.Tk[:, :], "dY", vTk)
    dma("s", T.yt[lo:hi, :], T.Tk[lo:hi, :], "oY1", vTk)
    send("stD", "landD", "arrD", tD)
    send("stY", "landY", "arrY", tY)
    tVR = dma("y", T.VR[:, :], T.landV[:], "dVR", ("arrV", 14), tV)
    tKD = dma("y", T.KD[:, :], T.landD[:], "dKD", ("arrD", 14), tD)
    m = MM([tKD], (T.pZ[:, :], T.R8b[:, :], T.KD[:, :], True, True))
    v = V(tt(T.YP[:, :], T.pZ[:, :], T.VR[:, :], A.max), m, tVR)
    dma("y", T.yp[:], T.YP[:, :], "oP", v)
    need("s", [("arrY", 14)])
    if me > 0:
        dma("s", T.yt[0:lo, :], T.landY[0:me], "oY2")
    if me < 7:
        dma("s", T.yt[hi:128, :], T.landY[me + 1:8], "oY2")
    need("g", [(s, n) for s, n in cnt.items() if n])
